import numpy as np
import ml_dtypes


def mxq(x, axis, fmt="e4m3"):
    dtype, down = {"e4m3": (ml_dtypes.float8_e4m3fn, 7), "e5m2": (ml_dtypes.float8_e5m2, 14)}[fmt]
    v = np.moveaxis(np.asarray(x, np.float32).astype(ml_dtypes.bfloat16).astype(np.float64), axis, -1)
    blocks = v.reshape(v.shape[:-1] + (-1, 32))
    amax = np.abs(blocks).max(-1, keepdims=True)
    byte = np.maximum(np.where(amax > 0, np.frexp(amax)[1] - 1 + 127, 0) - down, 1)
    scale = np.exp2(byte - 127.0)
    codes = (blocks / scale).astype(np.float32).astype(dtype).astype(np.float64)
    return np.moveaxis((codes * scale).reshape(v.shape), -1, axis)


WIDE = False


def mx_kscale(k):
    if not WIDE:
        return np.ones(k)
    levels = np.array([10, -10, 5, -5, 0])
    if k % 512:
        return np.exp2(np.random.permutation(np.resize(levels, k // 32))).repeat(32)
    a = np.empty((k // 512, 16))
    for p in range(k // 512):
        a[p, :8] = np.random.permutation(np.resize(levels, 8))
        for g in range(8):
            far = levels[np.abs(levels - a[p, g]) >= 10]
            a[p, g + 8] = far[np.random.randint(len(far))]
    return np.exp2(a.ravel()).repeat(32)


BF16 = ml_dtypes.bfloat16


def bf(x):
    return np.asarray(x, np.float32).astype(BF16)


def f64(x):
    return np.asarray(x).astype(np.float64)


E2M1 = np.array([0.0, 0.5, 1.0, 1.5, 2.0, 3.0, 4.0, 6.0, -0.0, -0.5, -1.0, -1.5, -2.0, -3.0, -4.0, -6.0])


def pack_weight(w, fmt):
    k, n = w.shape
    w = f64(bf(w)).reshape(k // 32, 32, n)
    amax = np.abs(w).max(1)
    if fmt == "e4m3":
        byte = np.frexp(amax)[1] - 1 + 127 - 7
    else:
        mant, ex = np.frexp(amax / 6.0)
        byte = np.where(mant > 0.5, ex, ex - 1) + 127
    byte = np.clip(np.where(amax > 0, byte, 1), 1, 254)
    scaled = (w * np.exp2(127.0 - byte)[:, None, :]).reshape(k, n).astype(np.float32)
    by_word = np.ascontiguousarray(scaled.reshape(k // 512, 128, 4, n).transpose(0, 1, 3, 2))
    if fmt == "e4m3":
        words = by_word.astype(ml_dtypes.float8_e4m3fn).view(np.uint8)
    else:
        c = by_word.astype(ml_dtypes.float4_e2m1fn).view(np.uint8) & 0xF
        words = c[..., 0::2] | (c[..., 1::2] << 4)
    return np.ascontiguousarray(words), np.ascontiguousarray(byte.astype(np.uint8).reshape(k // 512, 16, n))


def unpack_weight(words, scales, fmt):
    g, p, n, _ = words.shape
    if fmt == "e4m3":
        vals = np.ascontiguousarray(words).view(ml_dtypes.float8_e4m3fn).astype(np.float64)
    else:
        nib = np.empty((g, p, n, 4), np.uint8)
        nib[..., 0::2] = words & 0xF
        nib[..., 1::2] = words >> 4
        vals = E2M1[nib]
    vals = vals * np.repeat(np.exp2(scales.astype(np.float64) - 127.0), 8, axis=1)[..., None]
    return vals.transpose(0, 1, 3, 2).reshape(g * 512, n)
def pack4(w):
    words, scales = pack_weight(w, "e2m1")
    return words.reshape(words.shape[0], 128, -1), scales


def unpack4(words, scales):
    return unpack_weight(words.reshape(words.shape[0], 128, -1, 2), scales, "e2m1")


def planes(Y):
    n, m = Y.shape
    b = f64(bf(Y)).reshape(n // 32, 32, m)
    amax = np.abs(b).max(1)
    byte = np.clip(np.where(amax > 0, np.frexp(amax)[1] - 1 + 127 - 7, 1), 1, 254)
    codes = (b * np.exp2(127.0 - byte)[:, None, :]).reshape(n, m).astype(np.float32).astype(ml_dtypes.float8_e4m3fn).view(np.uint8)
    words = codes.reshape(n // 512, 128, 4, m).transpose(0, 1, 3, 2)
    return np.ascontiguousarray(words), np.ascontiguousarray(byte.astype(np.uint8).reshape(n // 512, 16, m))


B, H, W, P, D, N = 4, 12, 16, 3072, 1536, 1024
M = B * H * W


def setup_inputs():
    r = np.random.randn
    s = mx_kscale(P)
    t = mx_kscale(D)
    x = r(P, M) * s[:, None]
    we = r(P, D) / np.sqrt(P) * t[None, :] / s[:, None]
    x_words, x_scales = pack_weight(x, "e4m3")
    we_words, we_scales = pack4(we)
    return {
        "x_words": x_words,
        "x_scales": x_scales,
        "we_words": we_words,
        "we_scales": we_scales,
        "row_pos": bf(0.5 * r(H, D) * t[None, :]),
        "col_pos": bf(0.5 * r(W, D) * t[None, :]),
        "wq": bf(r(D, N) / np.sqrt(D) / t[:, None]),
        "bq": bf(0.3 * r(N)),
        "q_gain": bf(np.exp(0.8 * r(N))),
    }


def reference(x_words, x_scales, we_words, we_scales, row_pos, col_pos, wq, bq, q_gain):
    X = unpack_weight(x_words, x_scales, "e4m3")
    WE = unpack4(we_words, we_scales)
    E = (X.T @ WE).reshape(B, H, W, D)
    E = E + f64(row_pos)[None, :, None, :] + f64(col_pos)[None, None, :, :]
    E = E.reshape(M, D)
    y = mxq(E, 1, "e4m3") @ mxq(f64(wq), 0, "e4m3")
    y = (y + f64(bq)[None, :]) * f64(q_gain)[None, :]
    Y = y.T
    words, scales = planes(Y)
    return y, words, scales

@@ -1,0 +1,460 @@
+from contextlib import ExitStack
+
+import concourse.mybir as mybir
+from concourse.masks import make_identity
+
+F32 = mybir.dt.float32
+BF16 = mybir.dt.bfloat16
+I32 = mybir.dt.int32
+U32 = mybir.dt.uint32
+U8 = mybir.dt.uint8
+FP8X4 = mybir.dt.float8_e4m3fn_x4
+FP4X4 = mybir.dt.float4_e2m1fn_x4
+ADD = mybir.AluOpType.add
+MULT = mybir.AluOpType.mult
+IDENT = mybir.ActivationFunctionType.Identity
+
+P = 128
+H, W = 12, 16
+M, PV, D, N = 768, 3072, 1536, 1024
+KP = PV // 512
+DG = D // 512
+NG = N // 512
+IMG = H * W
+WIDE = 512
+NARROW = 128
+
+FLOPS = 2 * M * PV * D + 2 * M * D * N
+
+
+def tile_patch_embed_query_planes_h2_kernel(
+    tc, x_words, x_scales, we_words, we_scales, row_pos, col_pos, wq, bq, q_gain, out_0, out_1, out_2
+):
+    nc = tc.nc
+    with ExitStack() as ctx:
+        keep = ctx.enter_context(tc.tile_pool(name="keep", bufs=1))
+        work = ctx.enter_context(tc.tile_pool(name="work", bufs=2))
+        psum = ctx.enter_context(tc.psum_pool(name="psum", bufs=1))
+        ctx.enter_context(tc.manual_schedule())
+
+        def kept(name, shape, dtype):
+            return keep.tile(shape, dtype, name=name, align_bytes=64)
+
+        def bank(b):
+            return psum.tile([P, 512], F32, name="bank%d" % b, tag="bank%d" % b)
+
+        xw_hbm = x_words.rearrange("g p m t -> p g (m t)").bitcast(I32)
+        xs_hbm = x_scales.bitcast(I32)
+        ww_hbm = we_words.rearrange("g p b -> p g b").bitcast(I32)
+        ws_hbm = we_scales.bitcast(I32)
+        yw_hbm = out_1.rearrange("g p m t -> g p (m t)").bitcast(I32)
+        ys_hbm = out_2.bitcast(I32)
+
+        xw_a = kept("xw_a", [P, KP, WIDE], U32)
+        xw_b = kept("xw_b", [P, KP, M - WIDE], U32)
+        xs_a = kept("xs_a", [P, KP, WIDE], U8)
+        xs_b = kept("xs_b", [P, KP, M - WIDE], U8)
+        ws_raw = [kept("ws_raw%d" % g, [P, KP, 512], U8) for g in range(DG)]
+        ws = [kept("ws%d" % g, [P, KP, 512], U8) for g in range(DG)]
+        ww = [kept("ww%d" % g, [P, KP, 1024], U8) for g in range(DG)]
+        ww_raw = {}
+        wq_raw = [kept("wq_raw%d" % g, [P, 4, N], BF16) for g in range(DG)]
+        wq_w = {(g, n): kept("wq_w%d%d" % (g, n), [P, 512], U32) for g in range(DG) for n in range(NG)}
+        wq_s = {(g, n): kept("wq_s%d%d" % (g, n), [P, 512], U8) for g in range(DG) for n in range(NG)}
+        widths = [WIDE, NARROW, NARROW]
+        starts = [0, WIDE, WIDE + NARROW]
+        e_w = {(c, g): kept("e_w%d%d" % (c, g), [P, widths[c]], U32) for c in range(3) for g in range(DG)}
+        e_s = {(c, g): kept("e_s%d%d" % (c, g), [P, widths[c]], U8) for c in range(3) for g in range(DG)}
+        y_w = [kept("y_w%d" % n, [P, M], U32) for n in range(NG)]
+        y_s = kept("y_s", [P, NG, M], U8)
+        pos_raw = kept("pos_raw", [P, DG, P], BF16)
+        pos_ord = kept("pos_ord", [P, DG, P], BF16)
+        pos_t = kept("pos_t", [P, DG, P], BF16)
+        pos_a = [kept("pos_a%d" % g, [P, 4, IMG], F32) for g in range(DG)]
+        pos_b = [kept("pos_b%d" % g, [P, IMG, 4], F32) for g in range(DG)]
+        bq_sb = kept("bq_sb", [P, NG, 4], BF16)
+        gain_sb = kept("gain_sb", [P, NG, 4], BF16)
+        gain = kept("gain", [P, NG * 4], F32)
+        shift = kept("shift", [P, NG * 4], F32)
+        ident = kept("ident", [P, P], F32)
+        staged = {}
+
+        def load_scales(dst, src, c0, c1):
+            for r in range(4):
+                nc.sync.dma_start(
+                    out=dst[r:P:32].bitcast(I32),
+                    in_=src[:, r:16:4, c0 // 4 : c1 // 4].rearrange("g q n -> q g n"),
+                )
+
+        def load_x(dst, g0, g1, m0, m1):
+            nc.sync.dma_start(out=dst[:, g0:g1, :].bitcast(I32), in_=xw_hbm[:, g0:g1, m0:m1])
+
+        def load_ww(d, g0, g1):
+            if d not in ww_raw:
+                ww_raw[d] = work.tile([P, KP, 1024], U8, name="ww_raw", align_bytes=64)
+            nc.sync.dma_start(
+                out=ww_raw[d][:, g0:g1, :].bitcast(I32), in_=ww_hbm[:, g0:g1, 256 * d : 256 * (d + 1)]
+            )
+
+        def load_wq(d):
+            rows = wq[512 * d : 512 * (d + 1), :].rearrange("(q t r) n -> t q r n", t=4, r=8)
+            for t in range(4):
+                nc.sync.dma_start(out=wq_raw[d][:, t, :], in_=rows[t])
+
+        def load_pos(queue, src, first):
+            for quad in range(4):
+                lo = 32 * quad + first
+                queue.dma_start(
+                    out=pos_raw[lo : lo + src.shape[0]],
+                    in_=src.rearrange("i (g u c) -> i g u c", g=DG, u=4)[:, :, quad, :],
+                )
+
+        def order_pass(d, g):
+            for dst, src, run in ((ww[d], ww_raw[d], 4), (ws[d], ws_raw[d], 2)):
+                nc.vector.tensor_copy(
+                    out=dst[:, g, :].bitcast(I32).rearrange("p (t q w) -> p t q w", t=4, w=run),
+                    in_=src[:, g, :].bitcast(I32).rearrange("p (q t w) -> p t q w", t=4, w=run),
+                )
+
+        def order_slot(d, t):
+            for dst, src, run in ((ww[d], ww_raw[d], 4), (ws[d], ws_raw[d], 2)):
+                nc.vector.tensor_copy(
+                    out=dst[:].bitcast(I32).rearrange("p g (t q w) -> p t g q w", t=4, w=run)[:, t],
+                    in_=src[:].bitcast(I32).rearrange("p g (q t w) -> p t g q w", t=4, w=run)[:, t],
+                )
+
+        def order_pos():
+            for d in range(DG):
+                nc.scalar.copy(
+                    out=pos_ord[:, d, :].rearrange("p (t a r) -> p t a r", t=4, r=8),
+                    in_=pos_raw[:, d, :].rearrange("p (a t r) -> p t a r", t=4, r=8),
+                )
+
+        def turn_pos(d):
+            nc.vector.transpose(out=pos_t[:, d, :], in_=pos_ord[:, d, :])
+
+        def sum_pos(d):
+            both = pos_t[:, d, :].rearrange("p (t i) -> p t i", t=4)
+            nc.vector.tensor_tensor(
+                out=pos_a[d][:].rearrange("p t (i j) -> p t i j", j=W),
+                in0=both[:, :, W : W + H].unsqueeze(3).to_broadcast([P, 4, H, W]),
+                in1=both[:, :, 0:W].unsqueeze(2).to_broadcast([P, 4, H, W]),
+                op=ADD,
+            )
+
+        def interleave_pos(d):
+            nc.scalar.copy(out=pos_b[d][:], in_=pos_a[d][:].rearrange("p t m -> p m t"))
+
+        def embed_pass(acc, d, t, g, c):
+            if c == 0:
+                words, scales = xw_a[:, g, :], xs_a[:, g, :]
+            else:
+                cols = slice(starts[c] - WIDE, starts[c] - WIDE + NARROW)
+                words, scales = xw_b[:, g, cols], xs_b[:, g, cols]
+            nc.tensor.matmul_mx(
+                out=acc,
+                lhsT=ww[d][:, g, 256 * t : 256 * (t + 1)].bitcast(FP4X4),
+                lhsT_scale=ws[d][:, g, P * t : P * (t + 1)],
+                rhs=words.bitcast(FP8X4),
+                rhs_scale=scales,
+                start=(g == 0),
+                stop=(g == KP - 1),
+            )
+
+        def embed_wide_pass(accs, d, g):
+            for t in range(4):
+                embed_pass(accs[t][:], d, t, g, 0)
+
+        def embed_wide_slot(acc, d, t):
+            for g in range(KP):
+                embed_pass(acc[:], d, t, g, 0)
+
+        def embed_narrow(acc, d, c):
+            for t in range(4):
+                for g in range(KP):
+                    embed_pass(acc[:, P * t : P * (t + 1)], d, t, g, c)
+
+        def add_pos_wide(acc, d, t):
+            if ("e", d) not in staged:
+                staged["e", d] = work.tile([P, 4, WIDE], F32, name="wide_f32", bufs=3)
+            dst = staged["e", d]
+            two = 2 * IMG
+            nc.vector.tensor_tensor(
+                out=dst[:, t, 0:two].rearrange("p (b m) -> p b m", b=2),
+                in0=acc[:, 0:two].rearrange("p (b m) -> p b m", b=2),
+                in1=pos_a[d][:, t : t + 1, :].to_broadcast([P, 2, IMG]),
+                op=ADD,
+            )
+            nc.vector.tensor_tensor(
+                out=dst[:, t, two:WIDE], in0=acc[:, two:WIDE], in1=pos_a[d][:, t, 0 : WIDE - two], op=ADD
+            )
+
+        def interleave(copy, key, src, width):
+            dst = work.tile([P, width, 4], BF16, name="mix%d" % width, align_bytes=64, bufs=3)
+            staged[key] = dst
+            copy(
+                out=dst[:].rearrange("p (c i) t -> p c t i", i=4),
+                in_=src[:].rearrange("p t (c i) -> p c t i", i=4),
+            )
+
+        def add_pos_narrow(acc, d, c):
+            dst = work.tile([P, NARROW, 4], BF16, name="mix%d" % NARROW, align_bytes=64, bufs=3)
+            staged["eb", c, d] = dst
+            sums = acc[:].rearrange("p (t m) -> p m t", t=4)
+            m = 0
+            while m < NARROW:
+                at = (starts[c] + m) % IMG
+                run = min(NARROW - m, IMG - at)
+                nc.vector.tensor_tensor(
+                    out=dst[:, m : m + run, :], in0=sums[:, m : m + run, :], in1=pos_b[d][:, at : at + run, :], op=ADD
+                )
+                m += run
+
+        def quantize(key, words, scales):
+            nc.vector.quantize_mx(
+                out=words.bitcast(FP8X4), scales=scales, in_=staged[key][:].rearrange("p m t -> p (m t)")
+            )
+
+        def quantize_e(c, d):
+            quantize(("eb", c, d), e_w[c, d][:], e_s[c, d][:])
+
+        def mix_wq(copy, d, n):
+            dst = work.tile([P, 512, 4], BF16, name="mix_wq", align_bytes=64, bufs=3)
+            staged["wq", d, n] = dst
+            copy(
+                out=dst[:].rearrange("p (t m) j -> p t m j", t=4),
+                in_=wq_raw[d][:, :, 512 * n : 512 * (n + 1)].rearrange("p j (m t) -> p t m j", t=4),
+            )
+
+        def quantize_wq(d, n):
+            quantize(("wq", d, n), wq_w[d, n][:], wq_s[d, n][:])
+
+        def project(acc, n, t, c, groups=range(DG)):
+            for d in groups:
+                nc.tensor.matmul_mx(
+                    out=acc,
+                    lhsT=wq_w[d, n][:, P * t : P * (t + 1)].bitcast(FP8X4),
+                    lhsT_scale=wq_s[d, n][:, P * t : P * (t + 1)],
+                    rhs=e_w[c, d][:].bitcast(FP8X4),
+                    rhs_scale=e_s[c, d][:],
+                    start=(d == 0),
+                    stop=(d == DG - 1),
+                )
+
+        def finish(acc, n, t, c, on_vector=False):
+            if ("y", c, n) not in staged:
+                if c == 0:
+                    staged["y", c, n] = work.tile([P, 4, WIDE], F32, name="wide_f32", bufs=3)
+                else:
+                    staged["y", c, n] = work.tile([P, 4, NARROW], F32, name="narrow_f32", bufs=4)
+            j = 4 * n + t
+            dst, times, plus = staged["y", c, n][:, t, :], gain[:, j : j + 1], shift[:, j : j + 1]
+            if on_vector:
+                nc.vector.tensor_scalar(out=dst, in0=acc, scalar1=times, scalar2=plus, op0=MULT, op1=ADD)
+            else:
+                nc.scalar.activation(out=dst, in_=acc, func=IDENT, bias=plus, scale=times)
+
+        def project_narrow(acc, n, c):
+            for t in range(4):
+                project(acc[:, P * t : P * (t + 1)], n, t, c)
+
+        def finish_narrow(acc, n, c):
+            for t in range(4):
+                finish(acc[:, P * t : P * (t + 1)], n, t, c)
+
+        def mix_y(c, n):
+            interleave(nc.vector.tensor_copy, ("yb", c, n), staged["y", c, n], widths[c])
+
+        def quantize_y(c, n):
+            cols = slice(starts[c], starts[c] + widths[c])
+            quantize(("yb", c, n), y_w[n][:, cols], y_s[:, n, cols])
+
+        def turn_y(acc, c, n, m):
+            for t in range(4):
+                nc.tensor.transpose(acc[:, P * t : P * (t + 1)], staged["y", c, n][:, t, m : m + P], ident[:])
+
+        def store_y(copy, acc, c, n, m):
+            rows = work.tile([P, 512], F32, name="rows", bufs=4)
+            copy(out=rows[:].rearrange("m (p t) -> m p t", t=4), in_=acc[:].rearrange("m (t p) -> m p t", t=4))
+            first = starts[c] + m
+            nc.sync.dma_start(out=out_0[first : first + P, 512 * n : 512 * (n + 1)], in_=rows[:])
+
+        def store_words(n, m0, m1):
+            nc.sync.dma_start(out=yw_hbm[n, :, m0:m1], in_=y_w[n][:, m0:m1].bitcast(I32))
+
+        def store_scales(m0, m1):
+            for quad in range(4):
+                nc.sync.dma_start(
+                    out=ys_hbm[:, 4 * quad : 4 * quad + 4, m0 // 4 : m1 // 4].rearrange("n r m -> r n m"),
+                    in_=y_s[32 * quad : 32 * quad + 4, :, m0:m1].bitcast(I32),
+                )
+
+        act_copy, dve_copy = nc.scalar.copy, nc.vector.tensor_copy
+
+        load_x(xw_a, 0, 1, 0, WIDE)
+        load_ww(0, 0, 1)
+        nc.gpsimd.memset(pos_raw[:], 0.0)
+        load_pos(nc.gpsimd, row_pos, W)
+        for plane in (xs_a, ws_raw[0], ws_raw[1], ws_raw[2], xs_b):
+            nc.vector.memset(plane[:].bitcast(I32), 0)
+        load_scales(xs_a, xs_hbm, 0, WIDE)
+        load_scales(ws_raw[0], ws_hbm, 0, 512)
+        for g0, g1 in ((1, 2), (2, 4), (4, 6)):
+            load_x(xw_a, g0, g1, 0, WIDE)
+            load_ww(0, g0, g1)
+            if g0 == 1:
+                load_pos(nc.scalar, col_pos, 0)
+        load_scales(ws_raw[1], ws_hbm, 512, 1024)
+        load_ww(1, 0, 3)
+        load_ww(1, 3, 6)
+        load_wq(0)
+        load_scales(ws_raw[2], ws_hbm, 1024, 1536)
+        order_pos()
+
+        accs = [bank(t) for t in range(4)]
+        for g in range(KP):
+            order_pass(0, g)
+            embed_wide_pass(accs, 0, g)
+            if g == 3:
+                for d in range(DG):
+                    turn_pos(d)
+                sum_pos(0)
+                interleave_pos(0)
+        load_ww(2, 0, KP)
+        load_wq(1)
+        load_wq(2)
+        load_scales(xs_b, xs_hbm, WIDE, M)
+        load_x(xw_b, 0, KP, WIDE, M)
+        nc.sync.dma_start(out=bq_sb[:], in_=bq.rearrange("(n p t) -> p n t", n=NG, t=4))
+        nc.sync.dma_start(out=gain_sb[:], in_=q_gain.rearrange("(n p t) -> p n t", n=NG, t=4))
+        for d in range(1, DG):
+            sum_pos(d)
+            interleave_pos(d)
+
+        accs1 = [bank(4 + t) for t in range(4)]
+        for g in range(KP):
+            order_pass(1, g)
+            embed_wide_pass(accs1, 1, g)
+        for t in range(4):
+            add_pos_wide(accs[t], 0, t)
+        mix_wq(act_copy, 0, 0)
+        interleave(act_copy, ("eb", 0, 0), staged["e", 0], WIDE)
+        mix_wq(dve_copy, 0, 1)
+        for t in range(4):
+            order_slot(2, t)
+        quantize_wq(0, 0)
+        quantize_wq(0, 1)
+
+        accs2 = [bank(t) for t in range(4)]
+        embed_wide_slot(accs2[0], 2, 0)
+        mix_wq(act_copy, 1, 0)
+        for t in range(4):
+            add_pos_wide(accs1[t], 1, t)
+        interleave(act_copy, ("eb", 0, 1), staged["e", 1], WIDE)
+        quantize_e(0, 0)
+        embed_wide_slot(accs2[1], 2, 1)
+        add_pos_wide(accs2[0], 2, 0)
+        add_pos_wide(accs2[1], 2, 1)
+        quantize_wq(1, 0)
+        embed_wide_slot(accs2[2], 2, 2)
+        add_pos_wide(accs2[2], 2, 2)
+        mix_wq(dve_copy, 2, 0)
+        embed_wide_slot(accs2[3], 2, 3)
+        add_pos_wide(accs2[3], 2, 3)
+        interleave(act_copy, ("eb", 0, 2), staged["e", 2], WIDE)
+        quantize_wq(2, 0)
+        quantize_e(0, 1)
+
+        narrow = [bank(4 + d) for d in range(DG)]
+        embed_narrow(narrow[0], 0, 1)
+        mix_wq(dve_copy, 1, 1)
+        mix_wq(act_copy, 2, 1)
+        nc.vector.memset(ident[:], 0.0)
+        make_identity(nc, ident[:], nomemset=True)
+        nc.vector.tensor_copy(out=gain[:], in_=gain_sb[:].rearrange("p n t -> p (n t)"))
+        add_pos_narrow(narrow[0], 0, 1)
+        nc.vector.tensor_tensor(out=shift[:], in0=bq_sb[:].rearrange("p n t -> p (n t)"), in1=gain[:], op=MULT)
+        embed_narrow(narrow[1], 1, 1)
+        quantize_e(0, 2)
+        quantize_wq(1, 1)
+        quantize_e(1, 0)
+        add_pos_narrow(narrow[1], 1, 1)
+        embed_narrow(narrow[2], 2, 1)
+        quantize_wq(2, 1)
+        quantize_e(1, 1)
+        add_pos_narrow(narrow[2], 2, 1)
+        last = [bank(7)]
+        embed_narrow(last[0], 0, 2)
+        quantize_e(1, 2)
+        add_pos_narrow(last[0], 0, 2)
+
+        for n, banks in ((0, (0, 1, 2, 3)), (1, (4, 5, 6, 7))):
+            for t in range(4):
+                acc = bank(banks[t])
+                project(acc[:], n, t, 0)
+                finish(acc[:], n, t, 0)
+            if n == 0:
+                quantize_e(2, 0)
+                mix_y(0, 0)
+        quantize_y(0, 0)
+        turned = [bank(t) for t in range(4)]
+        for i in range(4):
+            turn_y(turned[i], 0, 0, P * i)
+        for i in range(4):
+            store_y(dve_copy if i % 2 == 0 else act_copy, turned[i], 0, 0, P * i)
+        mix_y(0, 1)
+
+        for n in range(NG):
+            acc = bank(4 + n)
+            project_narrow(acc, n, 1)
+            finish_narrow(acc, n, 1)
+        quantize_y(0, 1)
+
+        last.append(bank(6))
+        embed_narrow(last[1], 1, 2)
+        mix_y(1, 0)
+        mix_y(1, 1)
+        quantize_y(1, 0)
+        store_words(0, 0, M - NARROW)
+        add_pos_narrow(last[1], 1, 2)
+        turned = [bank(t) for t in range(4)]
+        for i in range(4):
+            turn_y(turned[i], 0, 1, P * i)
+        quantize_y(1, 1)
+        quantize_e(2, 1)
+        store_words(1, 0, M - NARROW)
+        store_scales(0, M - NARROW)
+        for i in range(4):
+            store_y(dve_copy if i == 1 else act_copy, turned[i], 0, 1, P * i)
+        last.append(bank(7))
+        embed_narrow(last[2], 2, 2)
+        add_pos_narrow(last[2], 2, 2)
+        quantize_e(2, 2)
+
+        turned = [bank(b) for b in (4, 5)]
+        for n in range(NG):
+            turn_y(turned[n], 1, n, 0)
+        first = [bank(t) for t in range(4)]
+        for t in range(4):
+            project(first[t][:, 0:P], 0, t, 2, range(DG - 1))
+        for n in range(NG):
+            store_y(act_copy, turned[n], 1, n, 0)
+        for t in range(4):
+            project(first[t][:, 0:P], 0, t, 2, range(DG - 1, DG))
+            finish(first[t][:, 0:P], 0, t, 2, t % 2 == 0)
+        for t, b in enumerate((6, 7, 4, 5)):
+            acc = bank(b)
+            project(acc[:, 0:P], 1, t, 2)
+            finish(acc[:, 0:P], 1, t, 2, t % 2 == 0)
+        turned = [bank(n) for n in range(NG)]
+        for n in range(NG):
+            turn_y(turned[n], 2, n, 0)
+        mix_y(2, 0)
+        quantize_y(2, 0)
+        store_words(0, M - NARROW, M)
+        mix_y(2, 1)
+        store_y(act_copy, turned[0], 2, 0, 0)
+        quantize_y(2, 1)
+        store_y(act_copy, turned[1], 2, 1, 0)
+        store_words(1, M - NARROW, M)
+        store_scales(M - NARROW, M)

@@ -22,6 +22,7 @@ DG = D // 512
 NG = N // 512
 IMG = H * W
 WIDE = 512
+REST = M - WIDE
 NARROW = 128
 
 FLOPS = 2 * M * PV * D + 2 * M * D * N
@@ -61,10 +62,10 @@ def tile_patch_embed_query_planes_h2_kernel(
         wq_raw = [kept("wq_raw%d" % g, [P, 4, N], BF16) for g in range(DG)]
         wq_w = {(g, n): kept("wq_w%d%d" % (g, n), [P, 512], U32) for g in range(DG) for n in range(NG)}
         wq_s = {(g, n): kept("wq_s%d%d" % (g, n), [P, 512], U8) for g in range(DG) for n in range(NG)}
-        widths = [WIDE, NARROW, NARROW]
-        starts = [0, WIDE, WIDE + NARROW]
-        e_w = {(c, g): kept("e_w%d%d" % (c, g), [P, widths[c]], U32) for c in range(3) for g in range(DG)}
-        e_s = {(c, g): kept("e_s%d%d" % (c, g), [P, widths[c]], U8) for c in range(3) for g in range(DG)}
+        widths = [WIDE, REST]
+        starts = [0, WIDE]
+        e_w = {(c, g): kept("e_w%d%d" % (c, g), [P, widths[c]], U32) for c in range(2) for g in range(DG)}
+        e_s = {(c, g): kept("e_s%d%d" % (c, g), [P, widths[c]], U8) for c in range(2) for g in range(DG)}
         y_w = [kept("y_w%d" % n, [P, M], U32) for n in range(NG)]
         y_s = kept("y_s", [P, NG, M], U8)
         pos_raw = kept("pos_raw", [P, DG, P], BF16)
@@ -145,12 +146,7 @@ def tile_patch_embed_query_planes_h2_kernel(
         def interleave_pos(d):
             nc.scalar.copy(out=pos_b[d][:], in_=pos_a[d][:].rearrange("p t m -> p m t"))
 
-        def embed_pass(acc, d, t, g, c):
-            if c == 0:
-                words, scales = xw_a[:, g, :], xs_a[:, g, :]
-            else:
-                cols = slice(starts[c] - WIDE, starts[c] - WIDE + NARROW)
-                words, scales = xw_b[:, g, cols], xs_b[:, g, cols]
+        def embed_pass(acc, d, t, g, words, scales):
             nc.tensor.matmul_mx(
                 out=acc,
                 lhsT=ww[d][:, g, 256 * t : 256 * (t + 1)].bitcast(FP4X4),
@@ -163,16 +159,17 @@ def tile_patch_embed_query_planes_h2_kernel(
 
         def embed_wide_pass(accs, d, g):
             for t in range(4):
-                embed_pass(accs[t][:], d, t, g, 0)
+                embed_pass(accs[t][:], d, t, g, xw_a[:, g, :], xs_a[:, g, :])
 
         def embed_wide_slot(acc, d, t):
             for g in range(KP):
-                embed_pass(acc[:], d, t, g, 0)
+                embed_pass(acc[:], d, t, g, xw_a[:, g, :], xs_a[:, g, :])
 
-        def embed_narrow(acc, d, c):
+        def embed_narrow(acc, d, h):
+            cols = slice(NARROW * h, NARROW * (h + 1))
             for t in range(4):
                 for g in range(KP):
-                    embed_pass(acc[:, P * t : P * (t + 1)], d, t, g, c)
+                    embed_pass(acc[:, P * t : P * (t + 1)], d, t, g, xw_b[:, g, cols], xs_b[:, g, cols])
 
         def add_pos_wide(acc, d, t):
             if ("e", d) not in staged:
@@ -197,13 +194,14 @@ def tile_patch_embed_query_planes_h2_kernel(
                 in_=src[:].rearrange("p t (c i) -> p c t i", i=4),
             )
 
-        def add_pos_narrow(acc, d, c):
-            dst = work.tile([P, NARROW, 4], BF16, name="mix%d" % NARROW, align_bytes=64, bufs=3)
-            staged["eb", c, d] = dst
+        def add_pos_narrow(acc, d, h):
+            if h == 0:
+                staged["eb", 1, d] = work.tile([P, REST, 4], BF16, name="mix%d" % REST, align_bytes=64, bufs=3)
+            dst = staged["eb", 1, d][:, NARROW * h : NARROW * (h + 1), :]
             sums = acc[:].rearrange("p (t m) -> p m t", t=4)
             m = 0
             while m < NARROW:
-                at = (starts[c] + m) % IMG
+                at = (WIDE + NARROW * h + m) % IMG
                 run = min(NARROW - m, IMG - at)
                 nc.vector.tensor_tensor(
                     out=dst[:, m : m + run, :], in0=sums[:, m : m + run, :], in1=pos_b[d][:, at : at + run, :], op=ADD
@@ -222,15 +220,15 @@ def tile_patch_embed_query_planes_h2_kernel(
             dst = work.tile([P, 512, 4], BF16, name="mix_wq", align_bytes=64, bufs=3)
             staged["wq", d, n] = dst
             copy(
-                out=dst[:].rearrange("p (t m) j -> p t m j", t=4),
-                in_=wq_raw[d][:, :, 512 * n : 512 * (n + 1)].rearrange("p j (m t) -> p t m j", t=4),
+                out=dst[:].rearrange("p (t m i) j -> p m t i j", t=4, i=2),
+                in_=wq_raw[d][:, :, 512 * n : 512 * (n + 1)].rearrange("p j (m i t) -> p m t i j", t=4, i=2),
             )
 
         def quantize_wq(d, n):
             quantize(("wq", d, n), wq_w[d, n][:], wq_s[d, n][:])
 
-        def project(acc, n, t, c, groups=range(DG)):
-            for d in groups:
+        def project(acc, n, t, c):
+            for d in range(DG):
                 nc.tensor.matmul_mx(
                     out=acc,
                     lhsT=wq_w[d, n][:, P * t : P * (t + 1)].bitcast(FP8X4),
@@ -246,21 +244,13 @@ def tile_patch_embed_query_planes_h2_kernel(
                 if c == 0:
                     staged["y", c, n] = work.tile([P, 4, WIDE], F32, name="wide_f32", bufs=3)
                 else:
-                    staged["y", c, n] = work.tile([P, 4, NARROW], F32, name="narrow_f32", bufs=4)
+                    staged["y", c, n] = work.tile([P, 4, REST], F32, name="rest_f32")
             j = 4 * n + t
             dst, times, plus = staged["y", c, n][:, t, :], gain[:, j : j + 1], shift[:, j : j + 1]
             if on_vector:
                 nc.vector.tensor_scalar(out=dst, in0=acc, scalar1=times, scalar2=plus, op0=MULT, op1=ADD)
             else:
                 nc.scalar.activation(out=dst, in_=acc, func=IDENT, bias=plus, scale=times)
-
-        def project_narrow(acc, n, c):
-            for t in range(4):
-                project(acc[:, P * t : P * (t + 1)], n, t, c)
-
-        def finish_narrow(acc, n, c):
-            for t in range(4):
-                finish(acc[:, P * t : P * (t + 1)], n, t, c)
 
         def mix_y(c, n):
             interleave(nc.vector.tensor_copy, ("yb", c, n), staged["y", c, n], widths[c])
@@ -274,7 +264,7 @@ def tile_patch_embed_query_planes_h2_kernel(
                 nc.tensor.transpose(acc[:, P * t : P * (t + 1)], staged["y", c, n][:, t, m : m + P], ident[:])
 
         def store_y(copy, acc, c, n, m):
-            rows = work.tile([P, 512], F32, name="rows", bufs=4)
+            rows = work.tile([P, 512], F32, name="rows", bufs=8)
             copy(out=rows[:].rearrange("m (p t) -> m p t", t=4), in_=acc[:].rearrange("m (t p) -> m p t", t=4))
             first = starts[c] + m
             nc.sync.dma_start(out=out_0[first : first + P, 512 * n : 512 * (n + 1)], in_=rows[:])
@@ -293,10 +283,9 @@ def tile_patch_embed_query_planes_h2_kernel(
 
         load_x(xw_a, 0, 1, 0, WIDE)
         load_ww(0, 0, 1)
-        nc.gpsimd.memset(pos_raw[:], 0.0)
-        load_pos(nc.gpsimd, row_pos, W)
-        for plane in (xs_a, ws_raw[0], ws_raw[1], ws_raw[2], xs_b):
+        for plane in (xs_a, ws_raw[0], pos_raw, ws_raw[1], ws_raw[2], xs_b):
             nc.vector.memset(plane[:].bitcast(I32), 0)
+        load_pos(nc.gpsimd, row_pos, W)
         load_scales(xs_a, xs_hbm, 0, WIDE)
         load_scales(ws_raw[0], ws_hbm, 0, 512)
         for g0, g1 in ((1, 2), (2, 4), (4, 6)):
@@ -315,11 +304,6 @@ def tile_patch_embed_query_planes_h2_kernel(
         for g in range(KP):
             order_pass(0, g)
             embed_wide_pass(accs, 0, g)
-            if g == 3:
-                for d in range(DG):
-                    turn_pos(d)
-                sum_pos(0)
-                interleave_pos(0)
         load_ww(2, 0, KP)
         load_wq(1)
         load_wq(2)
@@ -327,23 +311,25 @@ def tile_patch_embed_query_planes_h2_kernel(
         load_x(xw_b, 0, KP, WIDE, M)
         nc.sync.dma_start(out=bq_sb[:], in_=bq.rearrange("(n p t) -> p n t", n=NG, t=4))
         nc.sync.dma_start(out=gain_sb[:], in_=q_gain.rearrange("(n p t) -> p n t", n=NG, t=4))
-        for d in range(1, DG):
-            sum_pos(d)
-            interleave_pos(d)
+        for d in range(DG):
+            turn_pos(d)
+        sum_pos(0)
+        interleave_pos(0)
 
         accs1 = [bank(4 + t) for t in range(4)]
         for g in range(KP):
             order_pass(1, g)
             embed_wide_pass(accs1, 1, g)
+            if g % 3 == 2:
+                sum_pos(1 + g // 3)
+                interleave_pos(1 + g // 3)
         for t in range(4):
             add_pos_wide(accs[t], 0, t)
         mix_wq(act_copy, 0, 0)
         interleave(act_copy, ("eb", 0, 0), staged["e", 0], WIDE)
-        mix_wq(dve_copy, 0, 1)
         for t in range(4):
             order_slot(2, t)
         quantize_wq(0, 0)
-        quantize_wq(0, 1)
 
         accs2 = [bank(t) for t in range(4)]
         embed_wide_slot(accs2[0], 2, 0)
@@ -365,96 +351,63 @@ def tile_patch_embed_query_planes_h2_kernel(
         quantize_wq(2, 0)
         quantize_e(0, 1)
 
-        narrow = [bank(4 + d) for d in range(DG)]
-        embed_narrow(narrow[0], 0, 1)
-        mix_wq(dve_copy, 1, 1)
-        mix_wq(act_copy, 2, 1)
+        def embed_rest(i, b, *between):
+            acc = bank(b)
+            embed_narrow(acc, i // 2, i % 2)
+            for step in between:
+                step()
+            add_pos_narrow(acc, i // 2, i % 2)
+
+        mix_wq(act_copy, 0, 1)
+        mix_wq(act_copy, 1, 1)
+        embed_rest(0, 4)
         nc.vector.memset(ident[:], 0.0)
         make_identity(nc, ident[:], nomemset=True)
         nc.vector.tensor_copy(out=gain[:], in_=gain_sb[:].rearrange("p n t -> p (n t)"))
-        add_pos_narrow(narrow[0], 0, 1)
+        embed_rest(1, 5, lambda: quantize_e(0, 2))
         nc.vector.tensor_tensor(out=shift[:], in0=bq_sb[:].rearrange("p n t -> p (n t)"), in1=gain[:], op=MULT)
-        embed_narrow(narrow[1], 1, 1)
-        quantize_e(0, 2)
-        quantize_wq(1, 1)
-        quantize_e(1, 0)
-        add_pos_narrow(narrow[1], 1, 1)
-        embed_narrow(narrow[2], 2, 1)
-        quantize_wq(2, 1)
-        quantize_e(1, 1)
-        add_pos_narrow(narrow[2], 2, 1)
-        last = [bank(7)]
-        embed_narrow(last[0], 0, 2)
-        quantize_e(1, 2)
-        add_pos_narrow(last[0], 0, 2)
+        embed_rest(2, 6, lambda: mix_wq(dve_copy, 2, 1), lambda: quantize_e(1, 0))
+        embed_rest(3, 7, lambda: quantize_wq(0, 1), lambda: quantize_wq(2, 1))
+        embed_rest(4, 4, lambda: quantize_e(1, 1), lambda: quantize_wq(1, 1))
 
-        for n, banks in ((0, (0, 1, 2, 3)), (1, (4, 5, 6, 7))):
+        def second(c, n, banks, vector_slots=()):
             for t in range(4):
-                acc = bank(banks[t])
-                project(acc[:], n, t, 0)
-                finish(acc[:], n, t, 0)
-            if n == 0:
-                quantize_e(2, 0)
-                mix_y(0, 0)
+                acc = bank(banks[t])[:, 0 : widths[c]]
+                project(acc, n, t, c)
+                finish(acc, n, t, c, t in vector_slots)
+
+        def turn(c, n, banks):
+            accs = [bank(b) for b in banks]
+            for i, acc in enumerate(accs):
+                turn_y(acc, c, n, P * i)
+            return accs
+
+        second(0, 0, (0, 1, 2, 3))
+        second(0, 1, (5, 6, 7, 4))
+        mix_y(0, 0)
+        turned = turn(0, 0, (0, 1, 2, 3))
         quantize_y(0, 0)
-        turned = [bank(t) for t in range(4)]
+        store_words(0, 0, WIDE)
         for i in range(4):
-            turn_y(turned[i], 0, 0, P * i)
+            store_y(act_copy, turned[i], 0, 0, P * i)
+        embed_rest(5, 5, lambda: mix_y(0, 1), lambda: quantize_y(0, 1))
+        store_words(1, 0, WIDE)
+        store_scales(0, WIDE)
+        turned = turn(0, 1, (6, 7, 4, 0))
+        quantize_e(1, 2)
         for i in range(4):
-            store_y(dve_copy if i % 2 == 0 else act_copy, turned[i], 0, 0, P * i)
-        mix_y(0, 1)
-
-        for n in range(NG):
-            acc = bank(4 + n)
-            project_narrow(acc, n, 1)
-            finish_narrow(acc, n, 1)
-        quantize_y(0, 1)
-
-        last.append(bank(6))
-        embed_narrow(last[1], 1, 2)
+            store_y(act_copy if i % 2 == 0 else dve_copy, turned[i], 0, 1, P * i)
+        second(1, 0, (1, 2, 3, 5))
+        second(1, 1, (6, 7, 4, 0))
         mix_y(1, 0)
-        mix_y(1, 1)
+        turned = turn(1, 0, (1, 2)) + turn(1, 1, (3, 5))
         quantize_y(1, 0)
-        store_words(0, 0, M - NARROW)
-        add_pos_narrow(last[1], 1, 2)
-        turned = [bank(t) for t in range(4)]
-        for i in range(4):
-            turn_y(turned[i], 0, 1, P * i)
+        store_words(0, WIDE, M)
+        store_y(dve_copy, turned[0], 1, 0, 0)
+        store_y(act_copy, turned[1], 1, 0, P)
+        mix_y(1, 1)
+        store_y(act_copy, turned[2], 1, 1, 0)
         quantize_y(1, 1)
-        quantize_e(2, 1)
-        store_words(1, 0, M - NARROW)
-        store_scales(0, M - NARROW)
-        for i in range(4):
-            store_y(dve_copy if i == 1 else act_copy, turned[i], 0, 1, P * i)
-        last.append(bank(7))
-        embed_narrow(last[2], 2, 2)
-        add_pos_narrow(last[2], 2, 2)
-        quantize_e(2, 2)
-
-        turned = [bank(b) for b in (4, 5)]
-        for n in range(NG):
-            turn_y(turned[n], 1, n, 0)
-        first = [bank(t) for t in range(4)]
-        for t in range(4):
-            project(first[t][:, 0:P], 0, t, 2, range(DG - 1))
-        for n in range(NG):
-            store_y(act_copy, turned[n], 1, n, 0)
-        for t in range(4):
-            project(first[t][:, 0:P], 0, t, 2, range(DG - 1, DG))
-            finish(first[t][:, 0:P], 0, t, 2, t % 2 == 0)
-        for t, b in enumerate((6, 7, 4, 5)):
-            acc = bank(b)
-            project(acc[:, 0:P], 1, t, 2)
-            finish(acc[:, 0:P], 1, t, 2, t % 2 == 0)
-        turned = [bank(n) for n in range(NG)]
-        for n in range(NG):
-            turn_y(turned[n], 2, n, 0)
-        mix_y(2, 0)
-        quantize_y(2, 0)
-        store_words(0, M - NARROW, M)
-        mix_y(2, 1)
-        store_y(act_copy, turned[0], 2, 0, 0)
-        quantize_y(2, 1)
-        store_y(act_copy, turned[1], 2, 1, 0)
-        store_words(1, M - NARROW, M)
-        store_scales(M - NARROW, M)
+        store_y(act_copy, turned[3], 1, 1, P)
+        store_words(1, WIDE, M)
+        store_scales(WIDE, M)

@@ -20,6 +20,7 @@ M, PV, D, N = 768, 3072, 1536, 1024
 KP = PV // 512
 DG = D // 512
 NG = N // 512
+EARLY = 2
 IMG = H * W
 WIDE = 512
 REST = M - WIDE
@@ -53,12 +54,16 @@ def tile_patch_embed_query_planes_h2_kernel(
 
         xw_a = kept("xw_a", [P, KP, WIDE], U32)
         xw_b = kept("xw_b", [P, KP, M - WIDE], U32)
-        xs_a = kept("xs_a", [P, KP, WIDE], U8)
-        xs_b = kept("xs_b", [P, KP, M - WIDE], U8)
-        ws_raw = [kept("ws_raw%d" % g, [P, KP, 512], U8) for g in range(DG)]
-        ws = [kept("ws%d" % g, [P, KP, 512], U8) for g in range(DG)]
-        ww = [kept("ww%d" % g, [P, KP, 1024], U8) for g in range(DG)]
-        ww_raw = {}
+        runs = (range(0, EARLY), range(EARLY, KP))
+        xs = [kept("xs%d" % h, [P, len(runs[h]), M], U8) for h in range(2)]
+        ws_raw = [kept("ws_raw%d" % h, [P, len(runs[h]), D], U8) for h in range(2)]
+
+        def of_pass(planes, g):
+            return planes[0][:, g, :] if g < EARLY else planes[1][:, g - EARLY, :]
+
+        ws = kept("ws", [P, KP, D], U8)
+        ww = kept("ww", [P, KP, 2 * D], U8)
+        ww_last = kept("ww_last", [P, KP, 1024], U8)
         wq_raw = [kept("wq_raw%d" % g, [P, 4, N], BF16) for g in range(DG)]
         wq_w = {(g, n): kept("wq_w%d%d" % (g, n), [P, 512], U32) for g in range(DG) for n in range(NG)}
         wq_s = {(g, n): kept("wq_s%d%d" % (g, n), [P, 512], U8) for g in range(DG) for n in range(NG)}
@@ -80,22 +85,18 @@ def tile_patch_embed_query_planes_h2_kernel(
         ident = kept("ident", [P, P], F32)
         staged = {}
 
-        def load_scales(dst, src, c0, c1):
-            for r in range(4):
-                nc.sync.dma_start(
-                    out=dst[r:P:32].bitcast(I32),
-                    in_=src[:, r:16:4, c0 // 4 : c1 // 4].rearrange("g q n -> q g n"),
-                )
+        def load_scales(h):
+            for dst, src in ((ws_raw[h], ws_hbm), (xs[h], xs_hbm)):
+                for r in range(4):
+                    nc.sync.dma_start(
+                        out=dst[r:P:32].bitcast(I32),
+                        in_=src[runs[h].start : runs[h].stop, r:16:4, :].rearrange("g q n -> q g n"),
+                    )
 
-        def load_x(dst, g0, g1, m0, m1):
-            nc.sync.dma_start(out=dst[:, g0:g1, :].bitcast(I32), in_=xw_hbm[:, g0:g1, m0:m1])
-
-        def load_ww(d, g0, g1):
-            if d not in ww_raw:
-                ww_raw[d] = work.tile([P, KP, 1024], U8, name="ww_raw", align_bytes=64)
-            nc.sync.dma_start(
-                out=ww_raw[d][:, g0:g1, :].bitcast(I32), in_=ww_hbm[:, g0:g1, 256 * d : 256 * (d + 1)]
-            )
+        def load_pass(g):
+            staged["ww", g] = work.tile([P, 512], I32, name="ww_raw", bufs=3)
+            nc.sync.dma_start(out=staged["ww", g][:], in_=ww_hbm[:, g, 0:512])
+            nc.sync.dma_start(out=xw_a[:, g, :].bitcast(I32), in_=xw_hbm[:, g, 0:WIDE])
 
         def load_wq(d):
             rows = wq[512 * d : 512 * (d + 1), :].rearrange("(q t r) n -> t q r n", t=4, r=8)
@@ -110,19 +111,22 @@ def tile_patch_embed_query_planes_h2_kernel(
                     in_=src.rearrange("i (g u c) -> i g u c", g=DG, u=4)[:, :, quad, :],
                 )
 
-        def order_pass(d, g):
-            for dst, src, run in ((ww[d], ww_raw[d], 4), (ws[d], ws_raw[d], 2)):
+        def order_pass(g):
+            pairs = (
+                (ww[:, g, 0:2048].bitcast(I32), staged["ww", g][:], 4),
+                (ws[:, g, :].bitcast(I32), of_pass(ws_raw, g).bitcast(I32), 2),
+            )
+            for dst, src, run in pairs:
                 nc.vector.tensor_copy(
-                    out=dst[:, g, :].bitcast(I32).rearrange("p (t q w) -> p t q w", t=4, w=run),
-                    in_=src[:, g, :].bitcast(I32).rearrange("p (q t w) -> p t q w", t=4, w=run),
+                    out=dst.rearrange("p (d t q w) -> p d t q w", t=4, q=16, w=run),
+                    in_=src.rearrange("p (d q t w) -> p d t q w", t=4, q=16, w=run),
                 )
 
-        def order_slot(d, t):
-            for dst, src, run in ((ww[d], ww_raw[d], 4), (ws[d], ws_raw[d], 2)):
-                nc.vector.tensor_copy(
-                    out=dst[:].bitcast(I32).rearrange("p g (t q w) -> p t g q w", t=4, w=run)[:, t],
-                    in_=src[:].bitcast(I32).rearrange("p g (q t w) -> p t g q w", t=4, w=run)[:, t],
-                )
+        def order_last(t):
+            nc.vector.tensor_copy(
+                out=ww[:, :, 2048:3072].bitcast(I32).rearrange("p g (t q w) -> p t g q w", t=4, w=4)[:, t],
+                in_=ww_last[:].bitcast(I32).rearrange("p g (q t w) -> p t g q w", t=4, w=4)[:, t],
+            )
 
         def order_pos():
             for d in range(DG):
@@ -144,32 +148,37 @@ def tile_patch_embed_query_planes_h2_kernel(
             )
 
         def interleave_pos(d):
-            nc.scalar.copy(out=pos_b[d][:], in_=pos_a[d][:].rearrange("p t m -> p m t"))
+            nc.scalar.copy(
+                out=pos_b[d][:].rearrange("p (c i) t -> p c t i", i=2),
+                in_=pos_a[d][:].rearrange("p t (c i) -> p c t i", i=2),
+            )
 
-        def embed_pass(acc, d, t, g, words, scales):
+        def embed_pass(acc, d, t, g, words, cols):
+            j = 4 * d + t
             nc.tensor.matmul_mx(
                 out=acc,
-                lhsT=ww[d][:, g, 256 * t : 256 * (t + 1)].bitcast(FP4X4),
-                lhsT_scale=ws[d][:, g, P * t : P * (t + 1)],
+                lhsT=ww[:, g, 256 * j : 256 * (j + 1)].bitcast(FP4X4),
+                lhsT_scale=ws[:, g, P * j : P * (j + 1)],
                 rhs=words.bitcast(FP8X4),
-                rhs_scale=scales,
+                rhs_scale=of_pass(xs, g)[:, cols],
                 start=(g == 0),
                 stop=(g == KP - 1),
             )
 
         def embed_wide_pass(accs, d, g):
             for t in range(4):
-                embed_pass(accs[t][:], d, t, g, xw_a[:, g, :], xs_a[:, g, :])
+                embed_pass(accs[t][:], d, t, g, xw_a[:, g, :], slice(0, WIDE))
 
         def embed_wide_slot(acc, d, t):
             for g in range(KP):
-                embed_pass(acc[:], d, t, g, xw_a[:, g, :], xs_a[:, g, :])
+                embed_pass(acc[:], d, t, g, xw_a[:, g, :], slice(0, WIDE))
 
         def embed_narrow(acc, d, h):
-            cols = slice(NARROW * h, NARROW * (h + 1))
+            lo = NARROW * h
+            cols = slice(WIDE + lo, WIDE + lo + NARROW)
             for t in range(4):
                 for g in range(KP):
-                    embed_pass(acc[:, P * t : P * (t + 1)], d, t, g, xw_b[:, g, cols], xs_b[:, g, cols])
+                    embed_pass(acc[:, P * t : P * (t + 1)], d, t, g, xw_b[:, g, lo : lo + NARROW], cols)
 
         def add_pos_wide(acc, d, t):
             if ("e", d) not in staged:
@@ -190,8 +199,8 @@ def tile_patch_embed_query_planes_h2_kernel(
             dst = work.tile([P, width, 4], BF16, name="mix%d" % width, align_bytes=64, bufs=3)
             staged[key] = dst
             copy(
-                out=dst[:].rearrange("p (c i) t -> p c t i", i=4),
-                in_=src[:].rearrange("p t (c i) -> p c t i", i=4),
+                out=dst[:].rearrange("p (c i) t -> p c t i", i=2),
+                in_=src[:].rearrange("p t (c i) -> p c t i", i=2),
             )
 
         def add_pos_narrow(acc, d, h):
@@ -264,7 +273,7 @@ def tile_patch_embed_query_planes_h2_kernel(
                 nc.tensor.transpose(acc[:, P * t : P * (t + 1)], staged["y", c, n][:, t, m : m + P], ident[:])
 
         def store_y(copy, acc, c, n, m):
-            rows = work.tile([P, 512], F32, name="rows", bufs=8)
+            rows = work.tile([P, 512], F32, name="rows", bufs=6)
             copy(out=rows[:].rearrange("m (p t) -> m p t", t=4), in_=acc[:].rearrange("m (t p) -> m p t", t=4))
             first = starts[c] + m
             nc.sync.dma_start(out=out_0[first : first + P, 512 * n : 512 * (n + 1)], in_=rows[:])
@@ -281,74 +290,69 @@ def tile_patch_embed_query_planes_h2_kernel(
 
         act_copy, dve_copy = nc.scalar.copy, nc.vector.tensor_copy
 
-        load_x(xw_a, 0, 1, 0, WIDE)
-        load_ww(0, 0, 1)
-        for plane in (xs_a, ws_raw[0], pos_raw, ws_raw[1], ws_raw[2], xs_b):
+        load_pass(0)
+        for plane in (ws_raw[0], xs[0], pos_raw, ws_raw[1], xs[1]):
             nc.vector.memset(plane[:].bitcast(I32), 0)
+        load_scales(0)
         load_pos(nc.gpsimd, row_pos, W)
-        load_scales(xs_a, xs_hbm, 0, WIDE)
-        load_scales(ws_raw[0], ws_hbm, 0, 512)
-        for g0, g1 in ((1, 2), (2, 4), (4, 6)):
-            load_x(xw_a, g0, g1, 0, WIDE)
-            load_ww(0, g0, g1)
-            if g0 == 1:
-                load_pos(nc.scalar, col_pos, 0)
-        load_scales(ws_raw[1], ws_hbm, 512, 1024)
-        load_ww(1, 0, 3)
-        load_ww(1, 3, 6)
-        load_wq(0)
-        load_scales(ws_raw[2], ws_hbm, 1024, 1536)
+        load_pass(1)
+        load_scales(1)
+        load_pass(2)
+        load_pos(nc.scalar, col_pos, 0)
         order_pos()
 
-        accs = [bank(t) for t in range(4)]
-        for g in range(KP):
-            order_pass(0, g)
-            embed_wide_pass(accs, 0, g)
-        load_ww(2, 0, KP)
+        accs = [[bank(4 * d + t) for t in range(4)] for d in range(2)]
+
+        def both_groups(g):
+            order_pass(g)
+            for d in range(2):
+                embed_wide_pass(accs[d], d, g)
+
+        both_groups(0)
+        load_pass(3)
+        both_groups(1)
+        load_pass(4)
+        both_groups(2)
+        load_pass(5)
+        nc.sync.dma_start(out=ww_last[:].bitcast(I32), in_=ww_hbm[:, :, 512:768])
+        load_wq(0)
         load_wq(1)
+        nc.sync.dma_start(out=xw_b[:].bitcast(I32), in_=xw_hbm[:, :, WIDE:M])
         load_wq(2)
-        load_scales(xs_b, xs_hbm, WIDE, M)
-        load_x(xw_b, 0, KP, WIDE, M)
         nc.sync.dma_start(out=bq_sb[:], in_=bq.rearrange("(n p t) -> p n t", n=NG, t=4))
         nc.sync.dma_start(out=gain_sb[:], in_=q_gain.rearrange("(n p t) -> p n t", n=NG, t=4))
+        both_groups(3)
         for d in range(DG):
             turn_pos(d)
         sum_pos(0)
         interleave_pos(0)
-
-        accs1 = [bank(4 + t) for t in range(4)]
-        for g in range(KP):
-            order_pass(1, g)
-            embed_wide_pass(accs1, 1, g)
-            if g % 3 == 2:
-                sum_pos(1 + g // 3)
-                interleave_pos(1 + g // 3)
-        for t in range(4):
-            add_pos_wide(accs[t], 0, t)
+        both_groups(4)
+        for d in range(1, DG):
+            sum_pos(d)
+            interleave_pos(d)
         mix_wq(act_copy, 0, 0)
-        interleave(act_copy, ("eb", 0, 0), staged["e", 0], WIDE)
+        both_groups(5)
         for t in range(4):
-            order_slot(2, t)
-        quantize_wq(0, 0)
-
-        accs2 = [bank(t) for t in range(4)]
-        embed_wide_slot(accs2[0], 2, 0)
+            order_last(t)
         mix_wq(act_copy, 1, 0)
+
         for t in range(4):
-            add_pos_wide(accs1[t], 1, t)
+            add_pos_wide(accs[0][t], 0, t)
+        interleave(act_copy, ("eb", 0, 0), staged["e", 0], WIDE)
+        accs2 = [bank(t) for t in range(4)]
+        for t in range(4):
+            embed_wide_slot(accs2[t], 2, t)
+        for t in range(4):
+            add_pos_wide(accs[1][t], 1, t)
         interleave(act_copy, ("eb", 0, 1), staged["e", 1], WIDE)
-        quantize_e(0, 0)
-        embed_wide_slot(accs2[1], 2, 1)
-        add_pos_wide(accs2[0], 2, 0)
-        add_pos_wide(accs2[1], 2, 1)
+        quantize_wq(0, 0)
+        for t in range(3):
+            add_pos_wide(accs2[t], 2, t)
         quantize_wq(1, 0)
-        embed_wide_slot(accs2[2], 2, 2)
-        add_pos_wide(accs2[2], 2, 2)
-        mix_wq(dve_copy, 2, 0)
-        embed_wide_slot(accs2[3], 2, 3)
         add_pos_wide(accs2[3], 2, 3)
         interleave(act_copy, ("eb", 0, 2), staged["e", 2], WIDE)
-        quantize_wq(2, 0)
+        quantize_e(0, 0)
+        mix_wq(dve_copy, 2, 0)
         quantize_e(0, 1)
 
         def embed_rest(i, b, *between):
@@ -358,17 +362,17 @@ def tile_patch_embed_query_planes_h2_kernel(
                 step()
             add_pos_narrow(acc, i // 2, i % 2)
 
-        mix_wq(act_copy, 0, 1)
         mix_wq(act_copy, 1, 1)
-        embed_rest(0, 4)
+        mix_wq(act_copy, 2, 1)
+        embed_rest(0, 4, lambda: quantize_wq(2, 0))
         nc.vector.memset(ident[:], 0.0)
         make_identity(nc, ident[:], nomemset=True)
         nc.vector.tensor_copy(out=gain[:], in_=gain_sb[:].rearrange("p n t -> p (n t)"))
         embed_rest(1, 5, lambda: quantize_e(0, 2))
         nc.vector.tensor_tensor(out=shift[:], in0=bq_sb[:].rearrange("p n t -> p (n t)"), in1=gain[:], op=MULT)
-        embed_rest(2, 6, lambda: mix_wq(dve_copy, 2, 1), lambda: quantize_e(1, 0))
-        embed_rest(3, 7, lambda: quantize_wq(0, 1), lambda: quantize_wq(2, 1))
-        embed_rest(4, 4, lambda: quantize_e(1, 1), lambda: quantize_wq(1, 1))
+        embed_rest(2, 6, lambda: mix_wq(dve_copy, 0, 1), lambda: quantize_e(1, 0))
+        embed_rest(3, 7, lambda: quantize_wq(0, 1), lambda: quantize_wq(1, 1))
+        embed_rest(4, 4, lambda: quantize_e(1, 1), lambda: quantize_wq(2, 1))
 
         def second(c, n, banks, vector_slots=()):
             for t in range(4):

from contextlib import ExitStack

import concourse.mybir as mybir
from concourse.masks import make_identity

F32 = mybir.dt.float32
BF16 = mybir.dt.bfloat16
I32 = mybir.dt.int32
U32 = mybir.dt.uint32
U8 = mybir.dt.uint8
FP8X4 = mybir.dt.float8_e4m3fn_x4
FP4X4 = mybir.dt.float4_e2m1fn_x4
ADD = mybir.AluOpType.add
MULT = mybir.AluOpType.mult
IDENT = mybir.ActivationFunctionType.Identity

P = 128
H, W = 12, 16
M, PV, D, N = 768, 3072, 1536, 1024
KP = PV // 512
DG = D // 512
NG = N // 512
EARLY = 2
IMG = H * W
WIDE = 512
REST = M - WIDE
NARROW = 128

FLOPS = 2 * M * PV * D + 2 * M * D * N


def tile_patch_embed_query_planes_h2_kernel(
    tc, x_words, x_scales, we_words, we_scales, row_pos, col_pos, wq, bq, q_gain, out_0, out_1, out_2
):
    nc = tc.nc
    with ExitStack() as ctx:
        keep = ctx.enter_context(tc.tile_pool(name="keep", bufs=1))
        work = ctx.enter_context(tc.tile_pool(name="work", bufs=2))
        psum = ctx.enter_context(tc.psum_pool(name="psum", bufs=1))
        ctx.enter_context(tc.manual_schedule())

        def kept(name, shape, dtype):
            return keep.tile(shape, dtype, name=name, align_bytes=64)

        def bank(b):
            return psum.tile([P, 512], F32, name="bank%d" % b, tag="bank%d" % b)

        xw_hbm = x_words.rearrange("g p m t -> p g (m t)").bitcast(I32)
        xs_hbm = x_scales.bitcast(I32)
        ww_hbm = we_words.rearrange("g p b -> p g b").bitcast(I32)
        ws_hbm = we_scales.bitcast(I32)
        yw_hbm = out_1.rearrange("g p m t -> g p (m t)").bitcast(I32)
        ys_hbm = out_2.bitcast(I32)

        xw_a = kept("xw_a", [P, KP, WIDE], U32)
        xw_b = kept("xw_b", [P, KP, M - WIDE], U32)
        runs = (range(0, EARLY), range(EARLY, KP))
        xs = [kept("xs%d" % h, [P, len(runs[h]), M], U8) for h in range(2)]
        ws_raw = [kept("ws_raw%d" % h, [P, len(runs[h]), D], U8) for h in range(2)]

        def of_pass(planes, g):
            return planes[0][:, g, :] if g < EARLY else planes[1][:, g - EARLY, :]

        ws = kept("ws", [P, KP, D], U8)
        ww = kept("ww", [P, KP, 2 * D], U8)
        ww_last = kept("ww_last", [P, KP, 1024], U8)
        wq_raw = [kept("wq_raw%d" % g, [P, 4, N], BF16) for g in range(DG)]
        wq_w = {(g, n): kept("wq_w%d%d" % (g, n), [P, 512], U32) for g in range(DG) for n in range(NG)}
        wq_s = {(g, n): kept("wq_s%d%d" % (g, n), [P, 512], U8) for g in range(DG) for n in range(NG)}
        widths = [WIDE, REST]
        starts = [0, WIDE]
        e_w = {(c, g): kept("e_w%d%d" % (c, g), [P, widths[c]], U32) for c in range(2) for g in range(DG)}
        e_s = {(c, g): kept("e_s%d%d" % (c, g), [P, widths[c]], U8) for c in range(2) for g in range(DG)}
        y_w = [kept("y_w%d" % n, [P, M], U32) for n in range(NG)]
        y_s = kept("y_s", [P, NG, M], U8)
        pos_raw = kept("pos_raw", [P, DG, P], BF16)
        pos_ord = kept("pos_ord", [P, DG, P], BF16)
        pos_t = kept("pos_t", [P, DG, P], BF16)
        pos_a = [kept("pos_a%d" % g, [P, 4, IMG], F32) for g in range(DG)]
        pos_b = [kept("pos_b%d" % g, [P, IMG, 4], F32) for g in range(DG)]
        bq_sb = kept("bq_sb", [P, NG, 4], BF16)
        gain_sb = kept("gain_sb", [P, NG, 4], BF16)
        gain = kept("gain", [P, NG * 4], F32)
        shift = kept("shift", [P, NG * 4], F32)
        ident = kept("ident", [P, P], F32)
        staged = {}

        def load_scales(h):
            for dst, src in ((ws_raw[h], ws_hbm), (xs[h], xs_hbm)):
                for r in range(4):
                    nc.sync.dma_start(
                        out=dst[r:P:32].bitcast(I32),
                        in_=src[runs[h].start : runs[h].stop, r:16:4, :].rearrange("g q n -> q g n"),
                    )

        def load_pass(g):
            staged["ww", g] = work.tile([P, 512], I32, name="ww_raw", bufs=3)
            nc.sync.dma_start(out=staged["ww", g][:], in_=ww_hbm[:, g, 0:512])
            nc.sync.dma_start(out=xw_a[:, g, :].bitcast(I32), in_=xw_hbm[:, g, 0:WIDE])

        def load_wq(d):
            rows = wq[512 * d : 512 * (d + 1), :].rearrange("(q t r) n -> t q r n", t=4, r=8)
            for t in range(4):
                nc.sync.dma_start(out=wq_raw[d][:, t, :], in_=rows[t])

        def load_pos(queue, src, first):
            for quad in range(4):
                lo = 32 * quad + first
                queue.dma_start(
                    out=pos_raw[lo : lo + src.shape[0]],
                    in_=src.rearrange("i (g u c) -> i g u c", g=DG, u=4)[:, :, quad, :],
                )

        def order_pass(g):
            pairs = (
                (ww[:, g, 0:2048].bitcast(I32), staged["ww", g][:], 4),
                (ws[:, g, :].bitcast(I32), of_pass(ws_raw, g).bitcast(I32), 2),
            )
            for dst, src, run in pairs:
                nc.vector.tensor_copy(
                    out=dst.rearrange("p (d t q w) -> p d t q w", t=4, q=16, w=run),
                    in_=src.rearrange("p (d q t w) -> p d t q w", t=4, q=16, w=run),
                )

        def order_last(t):
            nc.vector.tensor_copy(
                out=ww[:, :, 2048:3072].bitcast(I32).rearrange("p g (t q w) -> p t g q w", t=4, w=4)[:, t],
                in_=ww_last[:].bitcast(I32).rearrange("p g (q t w) -> p t g q w", t=4, w=4)[:, t],
            )

        def order_pos():
            for d in range(DG):
                nc.scalar.copy(
                    out=pos_ord[:, d, :].rearrange("p (t a r) -> p t a r", t=4, r=8),
                    in_=pos_raw[:, d, :].rearrange("p (a t r) -> p t a r", t=4, r=8),
                )

        def turn_pos(d):
            nc.vector.transpose(out=pos_t[:, d, :], in_=pos_ord[:, d, :])

        def sum_pos(d):
            both = pos_t[:, d, :].rearrange("p (t i) -> p t i", t=4)
            nc.vector.tensor_tensor(
                out=pos_a[d][:].rearrange("p t (i j) -> p t i j", j=W),
                in0=both[:, :, W : W + H].unsqueeze(3).to_broadcast([P, 4, H, W]),
                in1=both[:, :, 0:W].unsqueeze(2).to_broadcast([P, 4, H, W]),
                op=ADD,
            )

        def interleave_pos(d):
            nc.scalar.copy(
                out=pos_b[d][:].rearrange("p (c i) t -> p c t i", i=2),
                in_=pos_a[d][:].rearrange("p t (c i) -> p c t i", i=2),
            )

        def embed_pass(acc, d, t, g, words, cols):
            j = 4 * d + t
            nc.tensor.matmul_mx(
                out=acc,
                lhsT=ww[:, g, 256 * j : 256 * (j + 1)].bitcast(FP4X4),
                lhsT_scale=ws[:, g, P * j : P * (j + 1)],
                rhs=words.bitcast(FP8X4),
                rhs_scale=of_pass(xs, g)[:, cols],
                start=(g == 0),
                stop=(g == KP - 1),
            )

        def embed_wide_pass(accs, d, g):
            for t in range(4):
                embed_pass(accs[t][:], d, t, g, xw_a[:, g, :], slice(0, WIDE))

        def embed_wide_slot(acc, d, t):
            for g in range(KP):
                embed_pass(acc[:], d, t, g, xw_a[:, g, :], slice(0, WIDE))

        def embed_narrow(acc, d, h):
            lo = NARROW * h
            cols = slice(WIDE + lo, WIDE + lo + NARROW)
            for t in range(4):
                for g in range(KP):
                    embed_pass(acc[:, P * t : P * (t + 1)], d, t, g, xw_b[:, g, lo : lo + NARROW], cols)

        def add_pos_wide(acc, d, t):
            if ("e", d) not in staged:
                staged["e", d] = work.tile([P, 4, WIDE], F32, name="wide_f32", bufs=3)
            dst = staged["e", d]
            two = 2 * IMG
            nc.vector.tensor_tensor(
                out=dst[:, t, 0:two].rearrange("p (b m) -> p b m", b=2),
                in0=acc[:, 0:two].rearrange("p (b m) -> p b m", b=2),
                in1=pos_a[d][:, t : t + 1, :].to_broadcast([P, 2, IMG]),
                op=ADD,
            )
            nc.vector.tensor_tensor(
                out=dst[:, t, two:WIDE], in0=acc[:, two:WIDE], in1=pos_a[d][:, t, 0 : WIDE - two], op=ADD
            )

        def interleave(copy, key, src, width):
            dst = work.tile([P, width, 4], BF16, name="mix%d" % width, align_bytes=64, bufs=3)
            staged[key] = dst
            copy(
                out=dst[:].rearrange("p (c i) t -> p c t i", i=2),
                in_=src[:].rearrange("p t (c i) -> p c t i", i=2),
            )

        def add_pos_narrow(acc, d, h):
            if h == 0:
                staged["eb", 1, d] = work.tile([P, REST, 4], BF16, name="mix%d" % REST, align_bytes=64, bufs=3)
            dst = staged["eb", 1, d][:, NARROW * h : NARROW * (h + 1), :]
            sums = acc[:].rearrange("p (t m) -> p m t", t=4)
            m = 0
            while m < NARROW:
                at = (WIDE + NARROW * h + m) % IMG
                run = min(NARROW - m, IMG - at)
                nc.vector.tensor_tensor(
                    out=dst[:, m : m + run, :], in0=sums[:, m : m + run, :], in1=pos_b[d][:, at : at + run, :], op=ADD
                )
                m += run

        def quantize(key, words, scales):
            nc.vector.quantize_mx(
                out=words.bitcast(FP8X4), scales=scales, in_=staged[key][:].rearrange("p m t -> p (m t)")
            )

        def quantize_e(c, d):
            quantize(("eb", c, d), e_w[c, d][:], e_s[c, d][:])

        def mix_wq(copy, d, n):
            dst = work.tile([P, 512, 4], BF16, name="mix_wq", align_bytes=64, bufs=3)
            staged["wq", d, n] = dst
            copy(
                out=dst[:].rearrange("p (t m i) j -> p m t i j", t=4, i=2),
                in_=wq_raw[d][:, :, 512 * n : 512 * (n + 1)].rearrange("p j (m i t) -> p m t i j", t=4, i=2),
            )

        def quantize_wq(d, n):
            quantize(("wq", d, n), wq_w[d, n][:], wq_s[d, n][:])

        def project(acc, n, t, c):
            for d in range(DG):
                nc.tensor.matmul_mx(
                    out=acc,
                    lhsT=wq_w[d, n][:, P * t : P * (t + 1)].bitcast(FP8X4),
                    lhsT_scale=wq_s[d, n][:, P * t : P * (t + 1)],
                    rhs=e_w[c, d][:].bitcast(FP8X4),
                    rhs_scale=e_s[c, d][:],
                    start=(d == 0),
                    stop=(d == DG - 1),
                )

        def finish(acc, n, t, c, on_vector=False):
            if ("y", c, n) not in staged:
                if c == 0:
                    staged["y", c, n] = work.tile([P, 4, WIDE], F32, name="wide_f32", bufs=3)
                else:
                    staged["y", c, n] = work.tile([P, 4, REST], F32, name="rest_f32")
            j = 4 * n + t
            dst, times, plus = staged["y", c, n][:, t, :], gain[:, j : j + 1], shift[:, j : j + 1]
            if on_vector:
                nc.vector.tensor_scalar(out=dst, in0=acc, scalar1=times, scalar2=plus, op0=MULT, op1=ADD)
            else:
                nc.scalar.activation(out=dst, in_=acc, func=IDENT, bias=plus, scale=times)

        def mix_y(c, n):
            interleave(nc.vector.tensor_copy, ("yb", c, n), staged["y", c, n], widths[c])

        def quantize_y(c, n):
            cols = slice(starts[c], starts[c] + widths[c])
            quantize(("yb", c, n), y_w[n][:, cols], y_s[:, n, cols])

        def turn_y(acc, c, n, m):
            for t in range(4):
                nc.tensor.transpose(acc[:, P * t : P * (t + 1)], staged["y", c, n][:, t, m : m + P], ident[:])

        def store_y(copy, acc, c, n, m):
            rows = work.tile([P, 512], F32, name="rows", bufs=6)
            copy(out=rows[:].rearrange("m (p t) -> m p t", t=4), in_=acc[:].rearrange("m (t p) -> m p t", t=4))
            first = starts[c] + m
            nc.sync.dma_start(out=out_0[first : first + P, 512 * n : 512 * (n + 1)], in_=rows[:])

        def store_words(n, m0, m1):
            nc.sync.dma_start(out=yw_hbm[n, :, m0:m1], in_=y_w[n][:, m0:m1].bitcast(I32))

        def store_scales(m0, m1):
            for quad in range(4):
                nc.sync.dma_start(
                    out=ys_hbm[:, 4 * quad : 4 * quad + 4, m0 // 4 : m1 // 4].rearrange("n r m -> r n m"),
                    in_=y_s[32 * quad : 32 * quad + 4, :, m0:m1].bitcast(I32),
                )

        act_copy, dve_copy = nc.scalar.copy, nc.vector.tensor_copy

        load_pass(0)
        for plane in (ws_raw[0], xs[0], pos_raw, ws_raw[1], xs[1]):
            nc.vector.memset(plane[:].bitcast(I32), 0)
        load_scales(0)
        load_pos(nc.gpsimd, row_pos, W)
        load_pass(1)
        load_scales(1)
        load_pass(2)
        load_pos(nc.scalar, col_pos, 0)
        order_pos()

        accs = [[bank(4 * d + t) for t in range(4)] for d in range(2)]

        def both_groups(g):
            order_pass(g)
            for d in range(2):
                embed_wide_pass(accs[d], d, g)

        both_groups(0)
        load_pass(3)
        both_groups(1)
        load_pass(4)
        both_groups(2)
        load_pass(5)
        nc.sync.dma_start(out=ww_last[:].bitcast(I32), in_=ww_hbm[:, :, 512:768])
        load_wq(0)
        load_wq(1)
        nc.sync.dma_start(out=xw_b[:].bitcast(I32), in_=xw_hbm[:, :, WIDE:M])
        load_wq(2)
        nc.sync.dma_start(out=bq_sb[:], in_=bq.rearrange("(n p t) -> p n t", n=NG, t=4))
        nc.sync.dma_start(out=gain_sb[:], in_=q_gain.rearrange("(n p t) -> p n t", n=NG, t=4))
        both_groups(3)
        for d in range(DG):
            turn_pos(d)
        sum_pos(0)
        interleave_pos(0)
        both_groups(4)
        for d in range(1, DG):
            sum_pos(d)
            interleave_pos(d)
        mix_wq(act_copy, 0, 0)
        both_groups(5)
        for t in range(4):
            order_last(t)
        mix_wq(act_copy, 1, 0)

        for t in range(4):
            add_pos_wide(accs[0][t], 0, t)
        interleave(act_copy, ("eb", 0, 0), staged["e", 0], WIDE)
        accs2 = [bank(t) for t in range(4)]
        for t in range(4):
            embed_wide_slot(accs2[t], 2, t)
        for t in range(4):
            add_pos_wide(accs[1][t], 1, t)
        interleave(act_copy, ("eb", 0, 1), staged["e", 1], WIDE)
        quantize_wq(0, 0)
        for t in range(3):
            add_pos_wide(accs2[t], 2, t)
        quantize_wq(1, 0)
        add_pos_wide(accs2[3], 2, 3)
        interleave(act_copy, ("eb", 0, 2), staged["e", 2], WIDE)
        quantize_e(0, 0)
        mix_wq(dve_copy, 2, 0)
        quantize_e(0, 1)

        def embed_rest(i, b, *between):
            acc = bank(b)
            embed_narrow(acc, i // 2, i % 2)
            for step in between:
                step()
            add_pos_narrow(acc, i // 2, i % 2)

        mix_wq(act_copy, 1, 1)
        mix_wq(act_copy, 2, 1)
        embed_rest(0, 4, lambda: quantize_wq(2, 0))
        nc.vector.memset(ident[:], 0.0)
        make_identity(nc, ident[:], nomemset=True)
        nc.vector.tensor_copy(out=gain[:], in_=gain_sb[:].rearrange("p n t -> p (n t)"))
        embed_rest(1, 5, lambda: quantize_e(0, 2))
        nc.vector.tensor_tensor(out=shift[:], in0=bq_sb[:].rearrange("p n t -> p (n t)"), in1=gain[:], op=MULT)
        embed_rest(2, 6, lambda: mix_wq(dve_copy, 0, 1), lambda: quantize_e(1, 0))
        embed_rest(3, 7, lambda: quantize_wq(0, 1), lambda: quantize_wq(1, 1))
        embed_rest(4, 4, lambda: quantize_e(1, 1), lambda: quantize_wq(2, 1))

        def second(c, n, banks, vector_slots=()):
            for t in range(4):
                acc = bank(banks[t])[:, 0 : widths[c]]
                project(acc, n, t, c)
                finish(acc, n, t, c, t in vector_slots)

        def turn(c, n, banks):
            accs = [bank(b) for b in banks]
            for i, acc in enumerate(accs):
                turn_y(acc, c, n, P * i)
            return accs

        second(0, 0, (0, 1, 2, 3))
        second(0, 1, (5, 6, 7, 4))
        mix_y(0, 0)
        turned = turn(0, 0, (0, 1, 2, 3))
        quantize_y(0, 0)
        store_words(0, 0, WIDE)
        for i in range(4):
            store_y(act_copy, turned[i], 0, 0, P * i)
        embed_rest(5, 5, lambda: mix_y(0, 1), lambda: quantize_y(0, 1))
        store_words(1, 0, WIDE)
        store_scales(0, WIDE)
        turned = turn(0, 1, (6, 7, 4, 0))
        quantize_e(1, 2)
        for i in range(4):
            store_y(act_copy if i % 2 == 0 else dve_copy, turned[i], 0, 1, P * i)
        second(1, 0, (1, 2, 3, 5))
        second(1, 1, (6, 7, 4, 0))
        mix_y(1, 0)
        turned = turn(1, 0, (1, 2)) + turn(1, 1, (3, 5))
        quantize_y(1, 0)
        store_words(0, WIDE, M)
        store_y(dve_copy, turned[0], 1, 0, 0)
        store_y(act_copy, turned[1], 1, 0, P)
        mix_y(1, 1)
        store_y(act_copy, turned[2], 1, 1, 0)
        quantize_y(1, 1)
        store_y(act_copy, turned[3], 1, 1, P)
        store_words(1, WIDE, M)
        store_scales(WIDE, M)
